import numpy as np, ml_dtypes
CORES = [0,7,8,15,16,23,24,31,32,39,40,47,48,55,56,63]
N = 16
T = 512
ROUTE = [[[10],[0],[12],[15],[12],[7],[9],[11],[9],[2],[8],[6],[8],[2],[2],[11],[1],[12],[1],[7],[11],[2],[11],[9],[12],[13],[3],[0],[11],[8],[7],[4],[6],[12],[7],[4],[14],[4],[12],[3],[8],[9],[9],[11],[7],[13],[8],[8],[5],[3],[15],[4],[13],[6],[9],[0],[4],[7],[13],[2],[12],[12],[9],[13],[4],[2],[10],[10],[14],[7],[14],[0],[13],[14],[10],[11],[14],[1],[6],[1],[9],[10],[10],[14],[3],[4],[7],[5],[2],[11],[11],[4],[3],[12],[12],[8],[4],[2],[7],[8],[9],[2],[15],[8],[3],[2],[15],[4],[11],[6],[9],[6],[15],[6],[8],[14],[1],[6],[10],[14],[8],[8],[2],[11],[10],[14],[7],[12],[8],[6],[2],[9],[4],[9],[15],[15],[10],[5],[0],[4],[10],[7],[3],[10],[12],[14],[10],[10],[9],[9],[2],[8],[14],[4],[5],[2],[7],[10],[5],[13],[8],[12],[0],[6],[14],[0],[9],[15],[5],[8],[1],[9],[12],[2],[7],[14],[12],[5],[0],[9],[13],[13],[3],[4],[6],[14],[2],[4],[6],[1],[11],[1],[3],[0],[8],[12],[14],[14],[14],[7],[15],[13],[14],[2],[7],[14],[8],[13],[14],[14],[7],[2],[6],[5],[1],[8],[8],[2],[1],[4],[6],[15],[13],[6],[13],[11],[1],[14],[3],[1],[0],[4],[9],[2],[15],[4],[8],[0],[15],[5],[5],[0],[4],[6],[6],[1],[7],[8],[9],[14],[7],[5],[9],[9],[12],[8],[3],[14],[7],[6],[9],[3],[5],[2],[5],[10],[3],[13],[0],[3],[11],[10],[0],[9],[8],[1],[15],[11],[0],[6],[15],[14],[12],[11],[12],[15],[14],[6],[1],[11],[1],[13],[13],[14],[4],[0],[5],[6],[11],[0],[13],[12],[11],[8],[14],[14],[10],[3],[3],[7],[3],[10],[6],[15],[12],[8],[1],[6],[0],[8],[13],[5],[0],[11],[12],[1],[3],[9],[12],[11],[2],[1],[9],[0],[11],[8],[13],[1],[14],[7],[14],[7],[0],[1],[12],[15],[0],[13],[7],[2],[15],[14],[11],[7],[15],[6],[13],[11],[6],[3],[6],[10],[9],[5],[12],[1],[13],[7],[3],[8],[15],[11],[7],[0],[7],[2],[14],[9],[8],[10],[0],[12],[8],[2],[14],[1],[10],[6],[11],[1],[10],[13],[14],[15],[5],[12],[7],[1],[13],[6],[10],[13],[8],[1],[0],[4],[3],[5],[2],[15],[2],[14],[9],[0],[5],[7],[12],[9],[5],[6],[14],[8],[4],[14],[8],[12],[5],[2],[1],[8],[5],[7],[1],[15],[7],[15],[3],[11],[11],[11],[11],[11],[12],[0],[3],[11],[8],[0],[0],[9],[15],[3],[9],[9],[0],[14],[0],[14],[2],[15],[7],[0],[14],[6],[3],[10],[14],[10],[11],[8],[15],[14],[6],[8],[7],[11],[7],[15],[8],[10],[8],[2],[7],[11],[2],[2],[14],[7],[2],[13],[2],[15],[12],[10],[12],[13],[14],[15],[10],[4],[1],[5],[5],[12],[3],[5],[15],[14],[11],[12],[9],[9]],[[1],[12],[2],[5],[6],[6],[7],[3],[7],[9],[11],[8],[14],[0],[10],[15],[2],[14],[4],[15],[10],[3],[8],[0],[8],[11],[13],[4],[3],[10],[11],[15],[7],[9],[15],[7],[7],[2],[11],[9],[6],[8],[8],[4],[7],[5],[12],[11],[9],[13],[0],[5],[9],[9],[12],[12],[4],[2],[14],[4],[6],[0],[14],[8],[14],[6],[1],[1],[5],[7],[1],[6],[10],[13],[8],[15],[5],[13],[7],[12],[4],[1],[2],[9],[0],[11],[6],[1],[4],[2],[5],[14],[11],[4],[1],[13],[4],[6],[13],[11],[11],[5],[0],[14],[13],[0],[5],[3],[5],[12],[10],[3],[15],[8],[7],[1],[8],[13],[12],[5],[15],[9],[12],[14],[11],[13],[2],[3],[1],[4],[11],[13],[11],[1],[3],[3],[8],[7],[7],[9],[11],[11],[14],[4],[8],[14],[7],[7],[14],[14],[9],[11],[4],[14],[5],[9],[14],[1],[15],[5],[7],[11],[12],[3],[5],[0],[13],[11],[6],[15],[9],[2],[14],[11],[2],[2],[15],[10],[6],[13],[11],[9],[4],[3],[13],[6],[6],[9],[11],[3],[5],[5],[1],[4],[0],[15],[1],[3],[2],[0],[12],[12],[1],[0],[5],[13],[11],[7],[12],[5],[7],[3],[8],[5],[3],[10],[9],[4],[12],[0],[11],[8],[3],[14],[12],[1],[11],[9],[13],[8],[9],[15],[8],[8],[1],[0],[5],[3],[6],[12],[0],[4],[6],[2],[2],[2],[3],[15],[7],[4],[15],[11],[0],[14],[14],[6],[14],[2],[6],[4],[9],[0],[5],[8],[10],[6],[7],[3],[2],[4],[0],[3],[5],[6],[5],[7],[11],[11],[1],[10],[15],[13],[13],[11],[11],[5],[15],[7],[7],[11],[7],[15],[1],[12],[9],[15],[14],[7],[12],[10],[12],[2],[12],[5],[3],[6],[4],[7],[12],[14],[6],[11],[11],[11],[9],[12],[5],[1],[14],[4],[11],[9],[11],[6],[9],[1],[15],[3],[4],[7],[0],[6],[7],[5],[12],[5],[14],[1],[3],[6],[10],[3],[14],[2],[13],[7],[6],[15],[4],[6],[11],[4],[14],[12],[12],[12],[13],[4],[13],[1],[9],[4],[8],[7],[7],[11],[6],[2],[2],[2],[5],[14],[2],[6],[15],[12],[1],[0],[11],[7],[3],[12],[15],[9],[10],[10],[1],[2],[11],[1],[10],[1],[10],[11],[5],[3],[4],[14],[8],[4],[5],[6],[0],[9],[2],[1],[3],[7],[12],[12],[15],[11],[9],[13],[1],[4],[10],[10],[12],[13],[2],[11],[8],[5],[15],[7],[6],[14],[0],[11],[13],[7],[7],[0],[4],[6],[5],[5],[7],[12],[2],[14],[0],[7],[14],[1],[2],[6],[10],[5],[14],[6],[5],[3],[3],[6],[2],[5],[12],[7],[5],[9],[10],[7],[8],[13],[10],[11],[10],[1],[11],[6],[13],[1],[0],[4],[14],[2],[9],[4],[2],[14],[10],[8],[1],[4],[8],[14],[7],[1],[11],[1],[8],[11],[10],[5],[13],[10],[9],[3],[9],[13],[11],[7],[6],[5],[2],[6],[7],[11],[8],[2]],[[0],[9],[12],[2],[6],[15],[15],[9],[1],[14],[4],[0],[15],[5],[9],[9],[14],[15],[0],[8],[1],[1],[5],[9],[13],[11],[13],[15],[0],[1],[14],[7],[7],[11],[4],[7],[6],[9],[9],[2],[14],[10],[14],[9],[4],[10],[0],[14],[8],[15],[3],[7],[13],[12],[13],[1],[6],[6],[11],[11],[0],[7],[3],[6],[2],[8],[0],[4],[10],[9],[10],[4],[1],[7],[10],[8],[14],[3],[2],[9],[14],[10],[6],[9],[10],[9],[1],[12],[8],[9],[0],[15],[11],[15],[13],[9],[6],[12],[4],[7],[4],[10],[2],[5],[7],[4],[7],[14],[9],[0],[10],[8],[4],[3],[0],[7],[4],[7],[4],[4],[9],[11],[8],[8],[9],[11],[5],[3],[14],[11],[15],[14],[8],[11],[9],[6],[2],[8],[14],[11],[6],[2],[10],[6],[9],[2],[14],[6],[13],[8],[12],[9],[7],[0],[4],[15],[5],[4],[10],[1],[8],[3],[13],[1],[4],[9],[7],[0],[11],[7],[0],[10],[1],[10],[0],[5],[4],[1],[15],[5],[1],[12],[8],[8],[14],[10],[8],[6],[13],[1],[10],[2],[7],[3],[14],[11],[14],[13],[13],[13],[6],[0],[7],[14],[2],[7],[10],[11],[10],[7],[13],[14],[7],[15],[2],[1],[5],[10],[11],[7],[13],[5],[10],[11],[13],[15],[6],[6],[6],[13],[3],[6],[5],[3],[10],[3],[11],[1],[0],[15],[8],[3],[11],[15],[5],[10],[8],[1],[5],[14],[6],[1],[5],[15],[3],[12],[14],[3],[11],[1],[13],[8],[12],[4],[14],[6],[5],[2],[15],[14],[9],[11],[8],[2],[11],[0],[7],[3],[11],[14],[1],[8],[14],[4],[15],[12],[2],[6],[13],[7],[7],[5],[10],[10],[0],[8],[15],[4],[9],[3],[2],[7],[6],[10],[7],[12],[13],[1],[10],[0],[7],[2],[13],[11],[0],[1],[0],[3],[1],[8],[3],[1],[10],[1],[2],[0],[7],[9],[0],[1],[4],[15],[7],[12],[3],[5],[8],[11],[13],[15],[10],[3],[5],[6],[3],[13],[4],[14],[6],[1],[5],[6],[4],[11],[11],[3],[11],[4],[8],[12],[15],[0],[7],[12],[8],[4],[15],[6],[8],[15],[9],[12],[12],[2],[6],[2],[12],[11],[6],[4],[2],[10],[2],[1],[4],[0],[5],[13],[0],[6],[3],[5],[11],[14],[2],[13],[15],[13],[0],[13],[5],[8],[5],[14],[1],[12],[11],[2],[14],[6],[0],[1],[3],[14],[14],[9],[2],[9],[9],[11],[10],[7],[9],[10],[5],[9],[2],[14],[2],[1],[8],[6],[12],[10],[0],[4],[12],[11],[2],[11],[4],[15],[14],[3],[14],[6],[0],[2],[11],[8],[5],[7],[7],[11],[14],[3],[3],[14],[14],[10],[4],[2],[1],[15],[13],[11],[6],[10],[4],[7],[3],[7],[0],[2],[10],[12],[14],[1],[11],[13],[2],[4],[8],[7],[13],[12],[10],[2],[4],[15],[13],[2],[2],[14],[5],[11],[5],[10],[14],[1],[14],[6],[14],[13],[8],[13],[15],[7],[14],[2],[13],[10]],[[0],[0],[13],[12],[4],[13],[6],[2],[0],[4],[13],[8],[11],[7],[4],[12],[7],[13],[7],[10],[11],[1],[3],[11],[14],[12],[15],[3],[13],[15],[4],[11],[13],[14],[12],[5],[1],[5],[9],[9],[5],[4],[8],[0],[4],[14],[15],[0],[13],[2],[11],[13],[10],[5],[9],[10],[12],[15],[10],[9],[12],[6],[9],[14],[3],[2],[15],[0],[8],[6],[8],[14],[10],[7],[9],[10],[13],[3],[7],[2],[4],[8],[7],[4],[3],[10],[4],[15],[11],[12],[9],[13],[12],[2],[6],[11],[9],[4],[1],[11],[4],[12],[7],[5],[3],[5],[3],[7],[5],[3],[1],[13],[6],[8],[6],[3],[6],[8],[0],[10],[12],[5],[3],[0],[5],[9],[2],[10],[2],[1],[9],[15],[13],[12],[10],[1],[12],[11],[15],[12],[13],[2],[1],[11],[1],[3],[12],[11],[8],[13],[0],[14],[11],[3],[14],[0],[11],[9],[11],[2],[0],[9],[10],[15],[11],[3],[14],[5],[0],[1],[0],[13],[11],[10],[14],[12],[9],[8],[3],[13],[2],[7],[15],[10],[15],[0],[12],[6],[12],[6],[1],[12],[8],[0],[14],[4],[4],[15],[7],[2],[2],[11],[2],[8],[8],[7],[3],[10],[11],[1],[15],[10],[6],[13],[5],[5],[15],[0],[9],[0],[1],[5],[8],[14],[9],[3],[3],[3],[5],[2],[0],[3],[14],[13],[0],[3],[8],[1],[14],[3],[0],[11],[8],[0],[0],[9],[12],[1],[3],[11],[0],[8],[2],[12],[7],[1],[13],[6],[8],[9],[1],[6],[3],[13],[8],[14],[11],[4],[0],[15],[15],[13],[11],[1],[12],[14],[8],[1],[5],[12],[2],[1],[1],[15],[7],[4],[8],[14],[15],[15],[3],[1],[2],[13],[0],[3],[10],[3],[3],[15],[6],[1],[12],[15],[12],[6],[8],[10],[3],[14],[3],[1],[2],[10],[4],[4],[2],[2],[12],[5],[4],[8],[12],[9],[12],[9],[8],[6],[13],[15],[15],[6],[1],[1],[0],[11],[10],[12],[4],[12],[15],[6],[13],[7],[8],[6],[6],[12],[10],[3],[14],[10],[9],[2],[13],[12],[1],[5],[13],[12],[2],[10],[13],[13],[11],[12],[3],[4],[3],[14],[4],[1],[0],[2],[5],[0],[7],[10],[7],[15],[7],[4],[6],[13],[15],[7],[4],[10],[10],[12],[4],[15],[6],[8],[8],[9],[5],[1],[7],[15],[3],[1],[1],[3],[11],[5],[4],[7],[13],[9],[7],[13],[0],[13],[9],[10],[8],[0],[9],[5],[0],[9],[2],[12],[5],[1],[2],[5],[14],[9],[0],[11],[13],[11],[0],[8],[8],[3],[5],[6],[13],[11],[12],[5],[15],[7],[5],[10],[0],[1],[14],[12],[5],[15],[12],[4],[4],[13],[5],[4],[6],[0],[15],[0],[14],[15],[8],[15],[15],[12],[5],[0],[2],[12],[4],[13],[4],[2],[6],[12],[8],[12],[15],[14],[2],[12],[12],[9],[12],[5],[12],[12],[14],[5],[9],[13],[3],[13],[2],[8],[6],[6],[2],[11],[1],[4],[12],[4],[9],[2],[3],[0]],[[10],[9],[8],[14],[7],[0],[4],[11],[1],[0],[14],[10],[13],[2],[6],[15],[14],[1],[8],[2],[7],[4],[7],[4],[11],[4],[1],[12],[0],[4],[9],[4],[12],[9],[6],[14],[14],[4],[7],[3],[6],[7],[7],[5],[4],[12],[0],[2],[5],[12],[0],[14],[15],[6],[13],[4],[5],[0],[6],[9],[6],[12],[7],[1],[8],[2],[7],[10],[8],[8],[12],[1],[14],[14],[0],[6],[6],[5],[5],[0],[14],[7],[10],[6],[1],[6],[3],[8],[12],[3],[2],[2],[12],[14],[8],[0],[3],[11],[13],[2],[8],[1],[14],[7],[15],[4],[1],[6],[9],[2],[8],[0],[2],[12],[10],[12],[8],[7],[5],[1],[0],[1],[14],[0],[9],[0],[10],[5],[8],[9],[6],[3],[10],[8],[13],[14],[5],[8],[15],[14],[12],[0],[0],[5],[13],[11],[9],[2],[0],[4],[4],[4],[8],[7],[11],[9],[1],[6],[14],[3],[2],[14],[1],[15],[1],[7],[9],[15],[4],[7],[6],[1],[15],[5],[8],[6],[11],[1],[2],[0],[4],[12],[15],[7],[14],[11],[8],[12],[5],[9],[13],[12],[5],[0],[13],[3],[3],[11],[11],[7],[6],[0],[2],[13],[12],[15],[7],[12],[10],[2],[2],[6],[15],[15],[10],[2],[13],[0],[2],[8],[11],[3],[1],[10],[6],[3],[11],[10],[14],[10],[7],[2],[1],[9],[7],[0],[5],[7],[11],[10],[6],[11],[4],[14],[3],[15],[12],[6],[15],[11],[0],[2],[6],[6],[5],[6],[11],[0],[14],[10],[11],[9],[12],[3],[6],[10],[0],[12],[4],[1],[8],[14],[11],[14],[9],[7],[4],[15],[15],[13],[6],[9],[12],[5],[7],[1],[1],[1],[15],[5],[12],[10],[14],[2],[0],[14],[6],[11],[0],[6],[0],[9],[9],[12],[4],[3],[15],[10],[3],[5],[12],[14],[0],[9],[7],[12],[0],[11],[1],[1],[4],[3],[11],[15],[9],[2],[8],[1],[0],[0],[1],[9],[2],[0],[12],[11],[4],[5],[0],[5],[11],[9],[6],[14],[3],[4],[8],[3],[9],[13],[11],[7],[14],[8],[6],[12],[7],[5],[9],[9],[8],[9],[2],[15],[10],[8],[11],[8],[12],[11],[9],[8],[6],[6],[8],[10],[12],[10],[9],[4],[9],[10],[3],[12],[3],[12],[14],[7],[10],[8],[14],[4],[9],[14],[1],[1],[9],[8],[8],[8],[10],[7],[11],[3],[11],[0],[6],[3],[1],[12],[2],[3],[0],[10],[10],[14],[6],[3],[13],[0],[9],[14],[0],[15],[14],[11],[10],[0],[9],[14],[5],[9],[10],[1],[2],[3],[11],[9],[7],[6],[5],[6],[6],[10],[0],[3],[10],[15],[7],[1],[0],[1],[1],[10],[2],[5],[2],[12],[5],[9],[9],[5],[14],[0],[9],[0],[4],[13],[14],[13],[6],[4],[12],[5],[11],[3],[10],[5],[3],[1],[15],[10],[5],[2],[10],[1],[9],[5],[1],[12],[14],[9],[11],[11],[9],[3],[1],[3],[12],[6],[3],[7],[11],[6],[4],[15],[6],[13],[9],[9],[12],[2]],[[13],[5],[5],[1],[1],[5],[0],[5],[6],[2],[4],[1],[5],[4],[8],[13],[10],[6],[3],[7],[7],[13],[5],[12],[5],[3],[7],[0],[13],[3],[12],[12],[3],[13],[13],[8],[6],[1],[2],[6],[8],[1],[14],[6],[0],[9],[4],[6],[10],[10],[7],[4],[15],[13],[13],[14],[7],[2],[1],[11],[11],[5],[5],[2],[8],[1],[8],[7],[10],[9],[12],[9],[10],[13],[2],[7],[7],[4],[1],[11],[2],[8],[0],[5],[15],[15],[10],[15],[7],[2],[8],[5],[15],[15],[8],[15],[12],[4],[11],[13],[15],[4],[14],[0],[3],[5],[11],[4],[6],[6],[1],[15],[1],[9],[9],[4],[2],[13],[15],[15],[5],[9],[4],[10],[9],[15],[4],[8],[10],[7],[9],[12],[12],[6],[3],[6],[2],[1],[12],[0],[15],[4],[11],[4],[0],[5],[4],[0],[3],[9],[9],[5],[2],[7],[10],[9],[7],[1],[8],[3],[5],[0],[3],[2],[4],[13],[2],[8],[2],[10],[12],[1],[15],[6],[14],[3],[10],[7],[2],[8],[13],[13],[14],[5],[0],[0],[2],[7],[13],[6],[12],[0],[3],[4],[7],[13],[15],[15],[0],[13],[12],[13],[13],[14],[15],[6],[14],[10],[1],[5],[6],[3],[9],[15],[9],[8],[0],[1],[8],[6],[5],[15],[10],[13],[6],[0],[11],[12],[8],[13],[8],[10],[12],[6],[4],[6],[0],[8],[7],[12],[0],[5],[3],[9],[5],[6],[8],[0],[5],[9],[10],[13],[12],[2],[4],[3],[15],[8],[14],[3],[1],[3],[5],[14],[10],[3],[15],[2],[2],[7],[13],[6],[8],[11],[15],[12],[7],[14],[14],[5],[7],[5],[13],[4],[5],[14],[8],[6],[15],[1],[4],[2],[3],[7],[7],[7],[11],[8],[13],[3],[0],[8],[12],[1],[6],[5],[12],[10],[12],[6],[4],[1],[7],[12],[10],[1],[1],[8],[6],[15],[5],[7],[10],[3],[11],[4],[14],[4],[6],[15],[4],[10],[7],[0],[8],[0],[10],[4],[9],[5],[0],[7],[13],[0],[4],[13],[0],[14],[1],[15],[5],[3],[10],[14],[2],[9],[14],[6],[0],[8],[10],[3],[6],[8],[15],[2],[3],[8],[7],[12],[10],[1],[8],[12],[8],[15],[13],[9],[5],[9],[6],[11],[9],[0],[9],[8],[15],[5],[2],[12],[14],[8],[10],[9],[3],[13],[10],[12],[0],[12],[2],[10],[11],[14],[9],[5],[4],[8],[3],[5],[5],[7],[13],[3],[4],[1],[3],[11],[0],[6],[12],[8],[9],[5],[10],[6],[0],[12],[14],[12],[0],[9],[5],[7],[2],[12],[3],[7],[2],[9],[0],[14],[9],[0],[8],[4],[4],[11],[3],[14],[14],[14],[15],[12],[5],[1],[3],[11],[1],[14],[10],[5],[14],[3],[4],[14],[2],[4],[1],[5],[1],[0],[13],[9],[7],[6],[4],[5],[12],[12],[7],[9],[13],[3],[15],[1],[11],[5],[14],[10],[5],[7],[1],[3],[7],[8],[3],[13],[5],[8],[13],[1],[12],[9],[0],[6],[1],[6],[9],[0],[11],[3]],[[2],[0],[3],[1],[3],[2],[6],[8],[4],[3],[11],[8],[14],[5],[10],[9],[2],[0],[0],[13],[4],[14],[10],[3],[8],[8],[7],[10],[15],[2],[14],[1],[5],[0],[10],[9],[12],[8],[12],[13],[8],[4],[8],[14],[7],[14],[10],[1],[2],[9],[13],[14],[4],[10],[7],[4],[1],[5],[11],[1],[8],[7],[15],[0],[10],[0],[2],[2],[11],[5],[4],[0],[3],[10],[11],[1],[0],[1],[10],[1],[10],[13],[14],[14],[12],[13],[12],[1],[12],[0],[9],[7],[0],[9],[11],[8],[14],[6],[12],[14],[4],[12],[8],[5],[15],[15],[9],[0],[5],[7],[0],[5],[9],[10],[3],[1],[7],[9],[7],[15],[13],[13],[7],[8],[15],[6],[11],[15],[3],[7],[10],[3],[9],[13],[15],[1],[4],[10],[0],[5],[1],[3],[13],[9],[15],[12],[11],[3],[9],[13],[9],[3],[1],[3],[4],[10],[15],[7],[4],[1],[15],[12],[15],[6],[4],[5],[13],[9],[14],[10],[0],[8],[15],[11],[12],[2],[4],[7],[11],[3],[15],[2],[6],[3],[5],[9],[6],[1],[8],[9],[2],[11],[15],[11],[7],[10],[14],[1],[12],[3],[14],[6],[15],[1],[14],[2],[9],[12],[9],[6],[5],[1],[8],[8],[7],[14],[10],[11],[4],[12],[4],[9],[3],[15],[1],[3],[14],[0],[9],[13],[3],[10],[15],[7],[12],[7],[8],[13],[3],[9],[6],[14],[8],[14],[8],[9],[10],[13],[5],[4],[10],[0],[9],[6],[9],[14],[9],[9],[0],[15],[9],[1],[11],[10],[9],[15],[12],[12],[3],[6],[13],[5],[1],[5],[3],[14],[0],[4],[14],[14],[14],[1],[13],[7],[13],[11],[1],[8],[10],[9],[0],[4],[4],[4],[3],[14],[5],[7],[8],[1],[0],[13],[8],[6],[12],[10],[7],[4],[12],[10],[4],[15],[1],[10],[12],[9],[1],[8],[4],[13],[0],[5],[11],[14],[13],[11],[1],[8],[5],[10],[3],[7],[6],[9],[1],[13],[9],[12],[12],[11],[2],[10],[12],[2],[8],[6],[5],[10],[9],[12],[15],[5],[12],[11],[9],[6],[13],[10],[5],[7],[2],[7],[1],[1],[4],[14],[10],[15],[6],[13],[4],[1],[13],[1],[13],[13],[11],[3],[9],[2],[3],[14],[8],[15],[1],[3],[15],[2],[14],[4],[15],[0],[13],[7],[7],[12],[2],[15],[11],[7],[9],[15],[7],[8],[7],[4],[2],[4],[6],[8],[14],[5],[1],[6],[6],[5],[4],[1],[13],[6],[15],[0],[9],[2],[14],[5],[9],[7],[10],[8],[4],[7],[1],[1],[3],[5],[6],[14],[11],[1],[9],[10],[9],[10],[1],[14],[13],[1],[8],[10],[4],[1],[12],[15],[12],[15],[3],[2],[1],[5],[1],[11],[13],[10],[5],[10],[9],[8],[1],[5],[6],[8],[14],[0],[10],[15],[6],[9],[4],[6],[11],[11],[3],[15],[9],[13],[0],[0],[2],[3],[2],[12],[5],[4],[8],[11],[15],[2],[5],[13],[2],[4],[10],[8],[15],[3],[10],[10],[2],[8],[8],[9]],[[9],[7],[13],[1],[13],[3],[4],[11],[12],[12],[0],[2],[5],[5],[2],[4],[14],[14],[8],[4],[7],[8],[10],[11],[2],[14],[10],[2],[1],[6],[7],[6],[1],[6],[15],[9],[14],[2],[0],[14],[13],[5],[3],[10],[13],[2],[0],[4],[7],[13],[9],[10],[3],[7],[15],[13],[2],[2],[6],[4],[13],[3],[13],[10],[0],[6],[3],[14],[4],[15],[0],[8],[11],[10],[3],[3],[6],[9],[4],[3],[14],[12],[13],[7],[2],[13],[13],[11],[3],[1],[12],[8],[14],[7],[13],[15],[13],[1],[10],[8],[5],[0],[14],[7],[14],[0],[11],[2],[12],[5],[13],[13],[2],[12],[13],[1],[11],[1],[0],[12],[12],[14],[1],[0],[9],[0],[10],[3],[5],[4],[1],[0],[4],[1],[5],[1],[2],[11],[15],[4],[1],[3],[6],[10],[15],[7],[0],[12],[14],[4],[0],[6],[11],[13],[12],[6],[5],[9],[7],[11],[13],[14],[8],[12],[3],[6],[10],[10],[5],[4],[9],[8],[9],[6],[6],[14],[1],[1],[6],[6],[15],[0],[8],[11],[9],[12],[4],[4],[11],[1],[0],[5],[15],[7],[9],[8],[7],[2],[12],[3],[0],[3],[9],[14],[11],[12],[9],[6],[6],[13],[0],[1],[7],[14],[11],[2],[7],[3],[2],[4],[14],[3],[4],[14],[4],[2],[14],[6],[12],[4],[15],[8],[7],[12],[8],[2],[11],[6],[2],[10],[10],[14],[14],[12],[13],[1],[13],[6],[5],[7],[6],[8],[10],[2],[14],[9],[12],[1],[0],[14],[2],[10],[3],[2],[14],[12],[5],[4],[9],[9],[7],[10],[11],[13],[6],[11],[7],[9],[9],[14],[11],[11],[7],[12],[5],[10],[10],[15],[3],[9],[8],[2],[14],[8],[6],[9],[10],[1],[12],[4],[1],[7],[4],[12],[10],[0],[14],[5],[0],[6],[0],[12],[12],[5],[12],[5],[13],[0],[13],[15],[14],[13],[4],[5],[5],[10],[0],[14],[5],[1],[10],[2],[2],[11],[14],[5],[11],[11],[6],[7],[13],[15],[3],[6],[8],[13],[15],[10],[7],[2],[3],[6],[4],[13],[11],[1],[15],[11],[13],[6],[6],[12],[14],[14],[14],[9],[15],[10],[9],[10],[11],[15],[15],[12],[6],[13],[2],[14],[8],[3],[11],[6],[2],[3],[13],[7],[8],[5],[12],[8],[10],[7],[10],[0],[9],[2],[0],[11],[8],[12],[4],[6],[11],[4],[2],[1],[12],[15],[14],[15],[11],[4],[10],[10],[9],[1],[15],[13],[7],[15],[7],[11],[12],[5],[12],[3],[15],[1],[3],[0],[4],[4],[3],[11],[10],[13],[2],[6],[14],[14],[12],[11],[8],[9],[4],[0],[6],[7],[10],[9],[0],[7],[11],[9],[15],[1],[12],[15],[13],[8],[12],[8],[2],[3],[5],[8],[6],[6],[1],[11],[13],[0],[9],[2],[1],[11],[8],[6],[9],[1],[9],[14],[12],[0],[7],[10],[9],[2],[15],[3],[13],[4],[3],[0],[5],[5],[13],[3],[4],[15],[10],[13],[13],[4],[7],[12],[1],[12],[13],[8],[10],[5]],[[15],[2],[8],[0],[1],[2],[4],[4],[7],[15],[15],[0],[7],[4],[11],[12],[15],[15],[15],[15],[1],[13],[9],[2],[1],[14],[10],[11],[2],[14],[13],[1],[11],[3],[7],[14],[4],[2],[0],[5],[4],[4],[6],[13],[12],[1],[0],[13],[13],[6],[13],[7],[9],[6],[11],[14],[2],[4],[6],[14],[12],[9],[6],[9],[8],[13],[6],[14],[9],[0],[14],[10],[12],[3],[2],[14],[2],[10],[11],[7],[2],[8],[14],[5],[12],[11],[7],[0],[9],[2],[1],[7],[3],[2],[12],[10],[3],[3],[2],[10],[15],[7],[3],[11],[0],[5],[15],[12],[1],[10],[7],[12],[7],[7],[8],[1],[2],[5],[14],[13],[3],[11],[12],[0],[9],[13],[3],[12],[15],[2],[11],[12],[10],[9],[12],[14],[7],[6],[1],[5],[5],[8],[11],[5],[14],[0],[4],[14],[15],[8],[6],[15],[2],[2],[0],[15],[15],[4],[9],[11],[6],[0],[11],[1],[15],[12],[13],[6],[9],[5],[5],[8],[0],[10],[4],[11],[1],[9],[5],[8],[15],[5],[15],[4],[10],[13],[8],[2],[12],[14],[6],[11],[9],[11],[2],[13],[12],[11],[1],[10],[10],[10],[14],[13],[7],[11],[13],[15],[1],[12],[2],[5],[13],[5],[6],[8],[11],[15],[9],[13],[10],[2],[3],[14],[0],[11],[6],[7],[10],[12],[10],[3],[6],[12],[1],[1],[14],[6],[4],[4],[10],[12],[8],[12],[5],[15],[0],[14],[6],[6],[12],[3],[4],[10],[6],[2],[0],[10],[1],[6],[3],[5],[6],[5],[4],[14],[5],[15],[7],[12],[1],[12],[6],[6],[9],[2],[2],[12],[15],[7],[9],[11],[9],[6],[13],[12],[14],[7],[12],[8],[8],[12],[5],[0],[0],[7],[12],[6],[4],[5],[2],[14],[6],[13],[4],[7],[12],[4],[14],[3],[10],[9],[12],[1],[0],[9],[9],[11],[10],[6],[4],[15],[14],[9],[12],[11],[6],[2],[6],[3],[11],[6],[3],[7],[7],[4],[5],[15],[12],[3],[12],[15],[12],[14],[9],[14],[14],[11],[0],[8],[2],[12],[15],[12],[3],[11],[4],[14],[13],[14],[14],[1],[7],[5],[9],[6],[5],[10],[7],[2],[3],[4],[6],[0],[11],[3],[2],[8],[6],[8],[15],[11],[1],[9],[11],[2],[13],[1],[0],[9],[15],[2],[15],[7],[7],[4],[15],[4],[12],[9],[13],[1],[3],[15],[5],[5],[10],[5],[6],[7],[10],[1],[4],[15],[2],[9],[3],[14],[12],[11],[15],[10],[4],[3],[8],[9],[8],[7],[11],[4],[4],[8],[1],[14],[14],[4],[1],[8],[11],[13],[10],[6],[14],[8],[11],[2],[13],[14],[14],[13],[13],[5],[5],[3],[14],[9],[15],[3],[13],[7],[15],[3],[12],[2],[13],[1],[12],[14],[5],[9],[14],[4],[8],[7],[14],[9],[2],[5],[6],[4],[15],[6],[3],[4],[7],[8],[9],[15],[15],[10],[8],[8],[0],[3],[5],[6],[12],[7],[0],[14],[5],[8],[0],[8],[12],[5],[8],[15],[7],[3],[11],[2]],[[5],[1],[6],[12],[8],[11],[3],[11],[0],[2],[9],[12],[8],[13],[14],[3],[13],[4],[2],[2],[8],[1],[0],[13],[6],[5],[0],[9],[15],[13],[8],[5],[11],[7],[3],[0],[9],[10],[14],[2],[9],[13],[8],[11],[9],[11],[3],[12],[13],[12],[2],[10],[12],[15],[0],[7],[9],[0],[2],[11],[1],[8],[14],[3],[6],[2],[11],[7],[8],[5],[0],[6],[6],[7],[13],[8],[11],[7],[3],[11],[14],[5],[8],[4],[2],[11],[9],[14],[2],[4],[9],[10],[10],[3],[7],[9],[6],[5],[10],[5],[13],[0],[6],[0],[2],[0],[4],[11],[14],[15],[8],[7],[6],[7],[10],[15],[14],[9],[4],[0],[3],[2],[12],[9],[8],[1],[7],[11],[8],[8],[15],[13],[4],[14],[14],[7],[13],[0],[12],[11],[13],[3],[3],[14],[0],[3],[2],[8],[0],[5],[13],[15],[4],[6],[12],[8],[8],[4],[7],[15],[2],[13],[13],[10],[13],[11],[12],[12],[11],[14],[0],[0],[10],[12],[7],[15],[14],[6],[12],[15],[4],[9],[10],[11],[3],[2],[7],[1],[0],[6],[0],[9],[13],[13],[6],[12],[8],[0],[3],[4],[12],[14],[2],[13],[4],[1],[15],[7],[11],[13],[10],[12],[14],[12],[4],[4],[4],[9],[9],[1],[12],[14],[6],[9],[10],[5],[2],[12],[6],[7],[9],[10],[15],[2],[14],[5],[5],[0],[1],[7],[0],[9],[8],[14],[5],[10],[10],[0],[7],[5],[9],[6],[8],[13],[8],[9],[1],[14],[11],[9],[5],[13],[5],[7],[5],[9],[14],[7],[12],[6],[8],[6],[13],[2],[1],[13],[15],[12],[3],[9],[1],[7],[1],[13],[6],[11],[7],[5],[5],[2],[15],[4],[12],[13],[6],[10],[6],[6],[15],[11],[13],[14],[6],[0],[2],[11],[4],[2],[13],[0],[14],[12],[0],[15],[9],[11],[6],[7],[0],[4],[14],[13],[7],[1],[11],[15],[8],[6],[13],[1],[14],[15],[13],[2],[11],[0],[8],[1],[5],[2],[2],[12],[10],[15],[1],[12],[6],[5],[0],[8],[8],[3],[11],[0],[12],[13],[15],[4],[7],[6],[0],[15],[15],[13],[14],[14],[10],[8],[8],[14],[5],[8],[10],[8],[3],[2],[4],[7],[14],[0],[12],[2],[0],[5],[12],[2],[8],[3],[8],[12],[7],[11],[1],[1],[12],[12],[5],[4],[13],[1],[7],[14],[10],[9],[6],[12],[4],[11],[1],[10],[3],[3],[13],[0],[11],[2],[11],[12],[13],[9],[4],[2],[7],[5],[0],[14],[4],[14],[5],[3],[11],[3],[6],[15],[5],[2],[15],[12],[7],[2],[1],[15],[6],[13],[0],[3],[15],[0],[4],[9],[8],[6],[8],[7],[11],[4],[2],[7],[0],[8],[11],[14],[12],[0],[8],[8],[14],[7],[9],[6],[9],[4],[2],[15],[8],[14],[2],[8],[5],[6],[5],[4],[1],[7],[5],[7],[4],[7],[12],[7],[13],[10],[2],[8],[1],[1],[14],[12],[10],[12],[12],[4],[5],[8],[2],[6],[15],[2],[0],[10],[13],[12]],[[0],[0],[11],[1],[3],[3],[10],[14],[9],[1],[6],[6],[9],[6],[4],[8],[8],[12],[1],[2],[10],[12],[5],[4],[11],[15],[12],[8],[5],[4],[1],[7],[1],[2],[3],[0],[11],[2],[14],[0],[9],[3],[9],[5],[13],[10],[10],[4],[13],[6],[2],[11],[12],[2],[15],[15],[4],[9],[15],[11],[10],[14],[13],[5],[4],[2],[1],[2],[5],[8],[6],[14],[5],[9],[11],[14],[9],[3],[1],[10],[11],[15],[10],[11],[5],[15],[11],[4],[8],[2],[3],[3],[1],[2],[6],[1],[0],[1],[5],[3],[11],[9],[8],[2],[3],[3],[9],[1],[0],[8],[2],[3],[14],[4],[12],[14],[7],[8],[9],[0],[7],[2],[4],[7],[14],[6],[9],[0],[1],[3],[12],[13],[8],[13],[11],[12],[7],[3],[5],[9],[3],[4],[9],[5],[2],[12],[11],[3],[0],[15],[11],[13],[7],[12],[11],[10],[1],[15],[12],[3],[14],[12],[6],[0],[7],[14],[2],[5],[9],[3],[0],[12],[10],[15],[2],[10],[9],[2],[0],[13],[5],[11],[14],[8],[14],[2],[7],[7],[6],[15],[9],[7],[9],[11],[8],[8],[0],[8],[3],[7],[2],[12],[12],[14],[7],[10],[14],[13],[5],[4],[6],[7],[13],[12],[14],[12],[12],[2],[0],[2],[10],[5],[1],[8],[7],[11],[12],[5],[9],[10],[1],[4],[3],[0],[11],[6],[13],[14],[3],[13],[8],[10],[15],[4],[5],[11],[8],[10],[5],[4],[3],[0],[8],[0],[0],[1],[2],[1],[8],[7],[15],[1],[7],[7],[14],[4],[10],[9],[1],[12],[2],[3],[7],[9],[10],[8],[15],[5],[4],[15],[8],[0],[1],[1],[3],[15],[11],[10],[15],[7],[9],[11],[10],[5],[11],[4],[0],[1],[9],[5],[5],[11],[5],[13],[10],[6],[3],[15],[5],[0],[4],[14],[11],[13],[11],[10],[9],[13],[3],[8],[7],[11],[7],[14],[7],[1],[6],[3],[3],[1],[15],[13],[15],[0],[2],[8],[6],[2],[9],[9],[7],[15],[1],[15],[1],[11],[0],[3],[9],[13],[2],[8],[0],[14],[14],[7],[9],[14],[10],[12],[10],[14],[0],[10],[10],[11],[1],[4],[2],[0],[12],[10],[0],[2],[15],[14],[10],[0],[13],[13],[3],[8],[7],[13],[8],[6],[13],[0],[14],[14],[4],[3],[0],[8],[10],[14],[5],[12],[4],[13],[7],[14],[2],[3],[13],[2],[0],[12],[7],[6],[3],[12],[11],[15],[8],[13],[5],[11],[7],[9],[4],[8],[0],[11],[2],[0],[10],[0],[14],[1],[10],[9],[2],[1],[13],[4],[9],[2],[9],[6],[15],[3],[3],[5],[13],[9],[14],[10],[8],[11],[0],[10],[2],[9],[5],[5],[1],[15],[1],[10],[6],[7],[10],[14],[12],[15],[7],[8],[8],[0],[3],[3],[15],[6],[10],[1],[13],[15],[14],[6],[12],[12],[11],[8],[4],[2],[8],[3],[4],[6],[1],[8],[9],[14],[8],[15],[14],[3],[2],[12],[15],[2],[6],[13],[13],[1],[4],[15],[3],[10],[0],[7]],[[5],[8],[9],[1],[5],[4],[14],[8],[12],[4],[3],[4],[3],[14],[12],[13],[10],[12],[3],[6],[12],[0],[6],[12],[5],[4],[4],[10],[2],[8],[0],[0],[8],[4],[2],[5],[2],[14],[4],[2],[9],[14],[14],[5],[11],[10],[13],[5],[10],[15],[2],[7],[13],[6],[1],[0],[4],[9],[11],[5],[0],[4],[4],[9],[4],[5],[13],[1],[12],[1],[8],[12],[12],[6],[1],[10],[2],[4],[7],[4],[4],[7],[11],[4],[10],[11],[10],[6],[6],[5],[9],[6],[10],[2],[8],[5],[5],[3],[1],[8],[2],[15],[6],[12],[9],[10],[3],[5],[9],[14],[11],[8],[9],[9],[12],[3],[4],[3],[1],[9],[10],[14],[14],[13],[12],[8],[15],[6],[11],[4],[0],[4],[6],[0],[1],[8],[7],[11],[14],[6],[13],[13],[1],[12],[15],[1],[8],[15],[5],[15],[15],[0],[2],[8],[4],[14],[4],[13],[8],[1],[6],[11],[10],[3],[7],[9],[9],[9],[12],[10],[4],[2],[13],[14],[9],[15],[4],[11],[15],[2],[1],[4],[5],[6],[8],[0],[12],[4],[1],[6],[6],[11],[14],[8],[13],[3],[8],[10],[14],[11],[0],[15],[11],[10],[7],[3],[2],[12],[2],[9],[14],[15],[14],[9],[9],[11],[10],[7],[7],[12],[12],[14],[11],[9],[6],[3],[9],[13],[12],[7],[12],[1],[10],[10],[6],[10],[1],[1],[8],[12],[0],[15],[2],[9],[5],[0],[5],[0],[7],[2],[7],[5],[0],[12],[3],[4],[0],[11],[1],[4],[5],[12],[9],[13],[2],[10],[10],[8],[6],[2],[5],[11],[12],[6],[6],[5],[4],[6],[1],[10],[11],[8],[9],[13],[12],[9],[6],[6],[2],[6],[12],[3],[14],[7],[2],[5],[0],[9],[7],[8],[0],[9],[11],[4],[4],[2],[3],[15],[6],[1],[9],[11],[5],[13],[14],[2],[11],[11],[3],[12],[10],[1],[14],[14],[12],[12],[14],[5],[15],[6],[12],[5],[2],[0],[15],[4],[6],[15],[11],[3],[8],[6],[0],[6],[5],[15],[2],[10],[4],[0],[5],[10],[12],[11],[4],[10],[1],[14],[15],[14],[14],[10],[11],[0],[10],[11],[9],[3],[14],[6],[0],[0],[13],[13],[11],[12],[3],[6],[0],[2],[9],[12],[2],[9],[8],[10],[15],[9],[11],[0],[4],[12],[2],[7],[0],[3],[2],[12],[5],[15],[0],[8],[11],[11],[7],[5],[8],[7],[1],[5],[12],[1],[10],[8],[8],[12],[7],[14],[7],[14],[11],[11],[15],[7],[5],[6],[7],[7],[14],[11],[11],[6],[3],[14],[2],[15],[2],[8],[0],[11],[12],[14],[12],[10],[5],[15],[2],[0],[6],[14],[0],[6],[14],[3],[3],[2],[1],[9],[0],[12],[9],[11],[13],[6],[10],[6],[10],[0],[3],[3],[10],[0],[4],[6],[10],[12],[0],[1],[9],[6],[9],[12],[15],[2],[7],[2],[7],[10],[1],[13],[9],[1],[10],[3],[8],[7],[12],[13],[12],[6],[14],[12],[12],[3],[2],[13],[7],[3],[12],[2],[12],[6]],[[10],[3],[12],[5],[5],[7],[0],[15],[0],[13],[11],[10],[14],[7],[2],[11],[5],[0],[14],[9],[8],[8],[5],[12],[7],[15],[3],[0],[1],[9],[7],[3],[0],[6],[6],[15],[14],[4],[11],[8],[5],[10],[6],[15],[2],[7],[9],[15],[2],[14],[15],[10],[2],[12],[8],[10],[7],[8],[14],[5],[5],[10],[2],[12],[1],[14],[3],[6],[5],[4],[0],[2],[6],[10],[5],[2],[6],[15],[7],[11],[11],[15],[7],[5],[6],[5],[8],[2],[12],[14],[0],[12],[10],[4],[6],[11],[6],[7],[14],[0],[2],[10],[3],[13],[6],[6],[0],[6],[11],[4],[12],[4],[5],[9],[10],[13],[7],[2],[1],[3],[13],[9],[10],[7],[10],[15],[1],[10],[7],[3],[6],[14],[0],[12],[14],[7],[9],[9],[7],[14],[4],[14],[8],[15],[15],[2],[7],[2],[13],[1],[0],[12],[15],[3],[7],[9],[8],[15],[3],[14],[3],[4],[10],[13],[12],[6],[14],[12],[10],[12],[3],[1],[0],[1],[2],[5],[9],[0],[5],[8],[9],[3],[4],[11],[0],[7],[6],[1],[5],[9],[6],[5],[15],[12],[13],[3],[2],[2],[6],[12],[3],[3],[14],[0],[15],[13],[0],[15],[8],[5],[11],[1],[12],[4],[8],[11],[14],[11],[15],[6],[11],[8],[0],[7],[15],[4],[9],[4],[13],[2],[10],[4],[5],[12],[1],[0],[5],[0],[3],[2],[15],[14],[13],[9],[2],[14],[12],[4],[11],[10],[4],[11],[0],[10],[14],[2],[9],[6],[13],[13],[10],[8],[0],[3],[6],[15],[5],[1],[5],[2],[8],[7],[6],[1],[12],[11],[11],[8],[10],[6],[3],[10],[8],[11],[4],[12],[10],[14],[3],[8],[5],[7],[13],[14],[10],[2],[12],[3],[3],[2],[4],[9],[9],[15],[6],[14],[10],[0],[11],[3],[1],[12],[15],[3],[0],[9],[13],[9],[15],[11],[0],[9],[15],[14],[12],[2],[4],[15],[15],[1],[0],[3],[9],[14],[7],[9],[1],[11],[4],[1],[1],[14],[12],[0],[1],[8],[11],[3],[5],[15],[9],[3],[7],[12],[12],[8],[11],[0],[6],[2],[0],[4],[11],[4],[4],[6],[0],[4],[1],[7],[6],[9],[5],[1],[13],[3],[11],[3],[7],[12],[13],[15],[1],[15],[13],[2],[11],[8],[1],[3],[5],[4],[8],[1],[9],[14],[7],[8],[4],[11],[14],[11],[7],[9],[2],[9],[0],[2],[14],[8],[9],[8],[6],[6],[12],[5],[3],[8],[13],[14],[14],[1],[4],[12],[12],[9],[2],[6],[15],[6],[9],[3],[5],[1],[3],[12],[0],[15],[14],[14],[0],[15],[1],[14],[13],[14],[2],[15],[11],[15],[13],[4],[12],[1],[15],[13],[7],[15],[4],[10],[14],[4],[6],[9],[12],[12],[5],[3],[12],[14],[12],[7],[1],[3],[12],[8],[10],[3],[13],[13],[5],[10],[8],[15],[12],[7],[12],[3],[0],[8],[2],[12],[10],[9],[4],[2],[0],[4],[15],[11],[8],[6],[7],[11],[5],[6],[3],[3],[2],[8],[15],[8]],[[11],[12],[2],[9],[6],[6],[3],[12],[1],[10],[4],[5],[4],[2],[11],[12],[13],[3],[10],[2],[6],[1],[8],[13],[12],[11],[5],[4],[7],[11],[7],[15],[13],[13],[14],[11],[9],[10],[9],[1],[12],[2],[13],[1],[13],[7],[4],[10],[7],[11],[8],[12],[0],[5],[11],[12],[13],[14],[10],[1],[1],[13],[12],[1],[14],[4],[7],[5],[6],[7],[0],[7],[15],[11],[12],[3],[6],[5],[10],[1],[14],[2],[11],[7],[15],[5],[2],[15],[13],[11],[7],[11],[0],[8],[3],[6],[4],[2],[0],[12],[15],[15],[1],[3],[11],[8],[3],[4],[1],[3],[7],[3],[11],[11],[9],[2],[15],[8],[0],[3],[2],[9],[0],[11],[15],[12],[0],[13],[12],[11],[7],[2],[0],[7],[0],[8],[0],[0],[15],[8],[2],[14],[4],[7],[9],[11],[9],[13],[4],[3],[9],[14],[2],[12],[9],[10],[14],[15],[4],[11],[10],[14],[5],[3],[9],[3],[6],[15],[9],[7],[10],[11],[11],[5],[2],[11],[1],[6],[14],[15],[10],[12],[4],[12],[13],[14],[13],[3],[15],[11],[8],[9],[5],[1],[3],[9],[1],[15],[15],[7],[2],[1],[1],[10],[0],[1],[8],[13],[1],[13],[12],[2],[9],[4],[4],[10],[8],[7],[1],[9],[11],[6],[1],[1],[1],[4],[9],[1],[14],[11],[7],[6],[7],[14],[5],[1],[6],[2],[12],[15],[6],[11],[1],[5],[0],[14],[0],[9],[10],[2],[10],[8],[2],[12],[15],[10],[3],[7],[5],[15],[5],[13],[0],[6],[4],[2],[8],[4],[13],[3],[8],[8],[8],[12],[3],[8],[6],[15],[4],[8],[7],[3],[6],[2],[9],[15],[15],[2],[4],[6],[7],[15],[14],[2],[8],[13],[8],[0],[9],[7],[2],[13],[5],[6],[15],[5],[12],[3],[11],[1],[2],[9],[6],[7],[8],[15],[14],[15],[13],[14],[6],[14],[12],[5],[7],[0],[13],[12],[0],[0],[14],[2],[0],[9],[3],[6],[13],[1],[8],[3],[9],[15],[0],[0],[6],[12],[2],[5],[9],[9],[3],[9],[2],[14],[1],[14],[14],[13],[15],[4],[13],[14],[0],[10],[2],[11],[2],[10],[13],[5],[3],[7],[4],[6],[4],[9],[4],[7],[0],[11],[15],[14],[1],[13],[12],[11],[5],[5],[7],[6],[11],[13],[2],[8],[14],[0],[15],[7],[11],[1],[10],[13],[2],[4],[0],[6],[1],[12],[5],[5],[8],[13],[11],[13],[13],[4],[7],[3],[4],[10],[4],[4],[14],[11],[14],[5],[8],[13],[2],[9],[7],[3],[2],[12],[6],[13],[9],[4],[3],[9],[8],[6],[2],[4],[15],[4],[6],[8],[13],[8],[4],[5],[3],[8],[7],[15],[10],[0],[3],[2],[13],[14],[7],[2],[4],[0],[6],[9],[4],[8],[8],[15],[13],[10],[8],[10],[10],[6],[7],[1],[15],[13],[4],[2],[8],[15],[12],[6],[5],[15],[6],[11],[3],[12],[13],[14],[7],[11],[2],[7],[3],[14],[12],[6],[0],[10],[9],[0],[14],[14],[15],[0]],[[13],[7],[12],[2],[5],[6],[15],[13],[12],[13],[7],[2],[5],[8],[0],[3],[13],[8],[4],[4],[15],[4],[4],[15],[14],[7],[15],[15],[11],[8],[2],[7],[7],[6],[1],[2],[12],[10],[13],[12],[10],[2],[9],[0],[3],[8],[5],[13],[13],[7],[4],[7],[12],[10],[13],[5],[4],[3],[2],[0],[1],[8],[1],[0],[1],[12],[8],[6],[5],[0],[7],[6],[10],[10],[8],[10],[7],[6],[2],[9],[3],[7],[3],[14],[0],[10],[2],[1],[4],[9],[15],[14],[13],[0],[3],[0],[13],[0],[1],[6],[5],[5],[2],[1],[7],[13],[0],[1],[3],[5],[7],[1],[15],[15],[9],[8],[5],[14],[8],[1],[6],[14],[1],[6],[1],[0],[13],[13],[1],[11],[8],[13],[13],[8],[15],[14],[10],[9],[13],[3],[7],[14],[10],[6],[14],[5],[5],[15],[14],[2],[1],[11],[4],[5],[7],[6],[7],[7],[7],[14],[8],[10],[2],[14],[4],[13],[14],[8],[6],[8],[14],[1],[9],[10],[8],[14],[3],[5],[7],[0],[5],[15],[12],[12],[11],[11],[13],[11],[13],[8],[12],[4],[13],[7],[4],[7],[9],[12],[14],[9],[13],[10],[3],[15],[7],[14],[8],[10],[11],[11],[6],[4],[12],[5],[3],[14],[13],[14],[3],[7],[6],[14],[0],[13],[6],[9],[2],[11],[11],[13],[3],[4],[1],[1],[14],[5],[8],[5],[1],[11],[8],[3],[10],[3],[3],[0],[9],[5],[3],[7],[1],[10],[15],[0],[6],[5],[1],[1],[3],[12],[10],[14],[0],[9],[13],[15],[10],[5],[9],[15],[14],[11],[13],[2],[1],[0],[10],[6],[6],[9],[1],[15],[13],[8],[2],[2],[10],[13],[13],[14],[4],[8],[13],[3],[3],[9],[4],[13],[8],[13],[13],[3],[8],[6],[12],[0],[14],[11],[15],[2],[5],[9],[10],[4],[12],[4],[8],[10],[15],[5],[12],[5],[5],[12],[11],[4],[0],[6],[1],[9],[7],[4],[9],[0],[14],[13],[11],[5],[9],[12],[14],[13],[8],[3],[11],[14],[2],[2],[8],[13],[1],[5],[10],[7],[11],[15],[11],[10],[5],[11],[15],[13],[12],[5],[6],[12],[10],[2],[14],[4],[6],[2],[5],[12],[4],[13],[6],[12],[0],[13],[10],[3],[11],[11],[5],[13],[10],[14],[15],[8],[13],[3],[13],[11],[5],[5],[3],[7],[2],[6],[11],[6],[6],[4],[6],[12],[13],[10],[3],[4],[15],[11],[6],[14],[3],[1],[11],[15],[1],[5],[13],[9],[3],[9],[13],[12],[2],[11],[14],[15],[12],[7],[15],[8],[11],[2],[15],[12],[7],[6],[9],[4],[10],[14],[4],[6],[1],[8],[15],[15],[2],[3],[9],[13],[13],[0],[11],[2],[4],[4],[7],[1],[9],[1],[3],[3],[2],[15],[6],[10],[1],[5],[7],[5],[0],[15],[4],[8],[14],[10],[1],[9],[6],[8],[6],[1],[6],[4],[11],[14],[0],[6],[14],[9],[7],[5],[12],[5],[9],[9],[7],[14],[10],[9],[4],[13],[3],[12],[4],[12],[1],[11]],[[0],[9],[3],[13],[12],[10],[3],[13],[5],[2],[8],[8],[2],[1],[7],[5],[9],[5],[4],[15],[15],[14],[0],[1],[1],[0],[2],[9],[14],[13],[5],[0],[11],[5],[2],[7],[1],[14],[10],[14],[6],[2],[2],[4],[12],[12],[14],[15],[2],[7],[15],[13],[3],[12],[15],[3],[4],[7],[0],[7],[7],[15],[13],[8],[11],[2],[0],[8],[10],[3],[6],[14],[14],[3],[7],[8],[1],[8],[4],[5],[10],[15],[14],[13],[13],[3],[9],[4],[5],[6],[2],[12],[3],[13],[0],[0],[5],[6],[14],[13],[8],[5],[0],[1],[9],[15],[7],[13],[7],[7],[9],[0],[4],[9],[1],[13],[9],[10],[15],[7],[3],[7],[14],[9],[6],[8],[5],[2],[8],[9],[7],[2],[1],[15],[4],[3],[11],[3],[2],[3],[5],[3],[5],[6],[4],[14],[10],[3],[1],[7],[5],[9],[5],[4],[8],[2],[12],[10],[1],[7],[7],[0],[13],[1],[0],[7],[14],[7],[9],[6],[4],[11],[7],[15],[6],[10],[3],[4],[11],[11],[4],[0],[10],[0],[7],[9],[1],[5],[1],[4],[0],[11],[14],[4],[3],[11],[9],[2],[5],[2],[15],[12],[3],[10],[5],[8],[5],[1],[12],[9],[0],[6],[14],[7],[13],[2],[5],[11],[7],[4],[6],[11],[4],[11],[6],[8],[12],[14],[5],[4],[14],[0],[11],[2],[10],[2],[4],[14],[11],[9],[10],[0],[10],[13],[1],[0],[15],[8],[10],[5],[6],[6],[8],[12],[7],[13],[7],[1],[13],[14],[12],[11],[9],[15],[7],[4],[2],[4],[8],[5],[13],[7],[12],[12],[8],[11],[6],[11],[2],[7],[12],[7],[3],[15],[4],[4],[8],[15],[4],[10],[7],[8],[1],[8],[2],[5],[0],[1],[11],[7],[12],[11],[7],[9],[1],[8],[11],[14],[3],[4],[15],[8],[3],[7],[0],[10],[12],[11],[7],[3],[9],[12],[9],[10],[14],[15],[9],[10],[8],[8],[10],[9],[12],[3],[3],[7],[2],[14],[14],[6],[10],[7],[6],[2],[2],[4],[13],[2],[1],[13],[9],[1],[15],[7],[8],[13],[0],[8],[4],[0],[8],[4],[2],[11],[8],[3],[6],[1],[13],[13],[5],[14],[2],[9],[3],[11],[3],[3],[5],[0],[3],[15],[14],[14],[14],[2],[9],[7],[7],[14],[2],[15],[9],[6],[13],[12],[7],[6],[0],[14],[15],[6],[6],[3],[12],[9],[2],[14],[5],[2],[11],[3],[6],[7],[6],[13],[11],[12],[3],[6],[1],[9],[6],[10],[11],[14],[14],[10],[15],[8],[13],[5],[6],[7],[14],[7],[11],[12],[9],[13],[0],[9],[3],[14],[3],[2],[11],[1],[13],[10],[7],[13],[14],[8],[15],[8],[13],[3],[9],[7],[7],[8],[14],[0],[3],[11],[3],[0],[1],[9],[9],[11],[9],[13],[10],[5],[8],[6],[5],[2],[12],[1],[6],[1],[3],[8],[5],[10],[1],[9],[0],[1],[4],[6],[14],[3],[10],[6],[7],[10],[11],[11],[5],[0],[7],[12],[7],[11],[12],[12],[10],[15]]]
YW = 561
def setup_inputs(rng):
    return {"x": rng.standard_normal((N, 128, T), dtype=np.float32).astype(ml_dtypes.bfloat16)}
def reference(x):
    y = np.full((N, 128, YW), np.nan, x.dtype)
    fill = [0] * N
    for r in range(N):
        for t in range(T):
            for e in ROUTE[r][t]:
                y[e][:, fill[e]] = x[r][:, t]
                fill[e] += 1
    return {"y": y}

@@ -1,0 +1,142 @@
+from concourse.bass import DstId, RemoteDMATransfer
+
+NTOK = 512
+YW = 561
+MAXB = 8
+
+SCRATCH = {
+    "xs": ("sbuf", [128, NTOK], "bfloat16"),
+    "pack": ("sbuf", [128, NTOK], "bfloat16"),
+    "land": ("sbuf", [128, YW], "bfloat16"),
+}
+SEMAPHORES = (["ld", "xin", "sent", "arr", "st"] + ["pg%d" % i for i in range(MAXB)]
+              + ["ph%d" % i for i in range(MAXB)])
+
+
+def _engines(mask):
+    return bin(mask).count("1")
+
+
+def _plan(T, topo):
+    route = T.tables["ROUTE"]
+    cores = list(T.cores)
+    n = len(cores)
+    toks = [[[] for _ in range(n)] for _ in range(n)]
+    for r in range(n):
+        for t, es in enumerate(route[r]):
+            toks[r][es[0]].append(t)
+    col = [[0] * n for _ in range(n)]
+    total = [0] * n
+    for e in range(n):
+        for r in range(n):
+            col[r][e] = total[e]
+            total[e] += len(toks[r][e])
+    teams, owner = [], []
+    for r in range(n):
+        c = cores[r]
+        base = c - c % 8
+        team = [k for k in range(base, base + 8) if topo.die(k) == topo.die(c)]
+        load = dict((k, 0) for k in team)
+        own = [None] * n
+
+        def can(k, e):
+            return k == cores[e] or topo.may_write(k, cores[e])
+
+        order = sorted(range(n), key=lambda e: (sum(can(k, e) for k in team), -len(toks[r][e]), e))
+        for e in order:
+            k = min((k for k in team if can(k, e)), key=lambda k: (load[k], k))
+            own[e] = k
+            load[k] += len(toks[r][e])
+        teams.append(team)
+        owner.append(own)
+    return cores, toks, col, total, teams, owner
+
+
+def _runs(ts):
+    out = []
+    for t in ts:
+        if out and out[-1][0] + out[-1][1] == t:
+            out[-1][1] += 1
+        else:
+            out.append([t, 1])
+    return out
+
+
+def rank_program(g, core, T, topo):
+    cores, toks, col, total, teams, owner = _plan(T, topo)
+    n = len(cores)
+    src = [r for r in range(n) if core in teams[r]]
+    if not src:
+        return
+    r = src[0]
+    lead = cores[r]
+    me = T.rank_of(core)
+    sem = T.sem
+    queues = [g.sync, g.scalar, g]
+    sent = 0
+
+    if core == lead:
+        g.sync.dma_start(T.xs[:], T.x[:]).then_inc(sem.ld, 16)
+        for q in queues:
+            q.wait_ge(sem.ld, 16)
+        helpers = [k for k in teams[r] if k != core]
+        ids = [DstId(rid=topo.addr(k)[0], pnc=topo.addr(k)[1]) for k in helpers]
+        g.remote_dma_fused([RemoteDMATransfer(dst_ids=ids, dma_engine_mask=0xFFFF, remote_sem=sem.xin,
+                                              srcs=[T.xs[:]], dsts=[T.xs[:] for _ in helpers])],
+                           local_sem=sem.sent)
+        sent += 16
+    else:
+        for q in queues:
+            q.wait_ge(sem.xin, 16)
+
+    mine = [e for e in range(n) if owner[r][e] == core and toks[r][e]]
+    mine.sort(key=lambda e: (cores[e] == core, topo.chip(cores[e]) == topo.chip(core), e))
+    blocks = []
+    pos, turn = 0, 0
+    for i, e in enumerate(mine):
+        ng = nh = 0
+        local = cores[e] == core
+        at = col[r][e] if local else pos
+        buf = T.land if local else T.pack
+        first = at
+        for t, ln in _runs(toks[r][e]):
+            q = queues[turn % 3]
+            turn += 1
+            if q is g:
+                q.dma_start(buf[:, at:at + ln], T.xs[:, t:t + ln]).then_inc(sem["pg%d" % i], 16)
+                ng += 1
+            else:
+                q.dma_start(buf[:, at:at + ln], T.xs[:, t:t + ln]).then_inc(sem["ph%d" % i], 16)
+                nh += 1
+            at += ln
+        if not local:
+            pos = at
+        blocks.append((e, first, ng, nh))
+
+    for i, (e, first, ng, nh) in enumerate(blocks):
+        if ng:
+            g.wait_ge(sem["pg%d" % i], 16 * ng)
+        if nh:
+            g.wait_ge(sem["ph%d" % i], 16 * nh)
+        dst = cores[e]
+        if dst == core:
+            continue
+        w = len(toks[r][e])
+        rid, pid, _se = topo.addr(dst)
+        m = topo.mask(core, dst)
+        g.remote_dma(T.land[:, col[r][e]:col[r][e] + w], T.pack[:, first:first + w],
+                     sem.arr, sem.sent, pid, rid, m)
+        sent += _engines(m)
+
+    if me is not None:
+        need = 0
+        for s in range(n):
+            k = owner[s][me]
+            if toks[s][me] and k != core:
+                need += _engines(topo.mask(k, core))
+        if need:
+            g.wait_ge(sem.arr, need)
+        g.dma_start(T.y[:, 0:total[me]], T.land[:, 0:total[me]]).then_inc(sem.st, 16)
+        g.wait_ge(sem.st, 16)
+    if sent:
+        g.wait_ge(sem.sent, sent)

@@ -2,7 +2,7 @@ from concourse.bass import DstId, RemoteDMATransfer
 
 NTOK = 512
 YW = 561
-MAXB = 8
+MAXB = 10
 
 SCRATCH = {
     "xs": ("sbuf", [128, NTOK], "bfloat16"),
@@ -12,47 +12,14 @@ SCRATCH = {
 SEMAPHORES = (["ld", "xin", "sent", "arr", "st"] + ["pg%d" % i for i in range(MAXB)]
               + ["ph%d" % i for i in range(MAXB)])
 
+CACHE = {}
 
-def _engines(mask):
+
+def engines(mask):
     return bin(mask).count("1")
 
 
-def _plan(T, topo):
-    route = T.tables["ROUTE"]
-    cores = list(T.cores)
-    n = len(cores)
-    toks = [[[] for _ in range(n)] for _ in range(n)]
-    for r in range(n):
-        for t, es in enumerate(route[r]):
-            toks[r][es[0]].append(t)
-    col = [[0] * n for _ in range(n)]
-    total = [0] * n
-    for e in range(n):
-        for r in range(n):
-            col[r][e] = total[e]
-            total[e] += len(toks[r][e])
-    teams, owner = [], []
-    for r in range(n):
-        c = cores[r]
-        base = c - c % 8
-        team = [k for k in range(base, base + 8) if topo.die(k) == topo.die(c)]
-        load = dict((k, 0) for k in team)
-        own = [None] * n
-
-        def can(k, e):
-            return k == cores[e] or topo.may_write(k, cores[e])
-
-        order = sorted(range(n), key=lambda e: (sum(can(k, e) for k in team), -len(toks[r][e]), e))
-        for e in order:
-            k = min((k for k in team if can(k, e)), key=lambda k: (load[k], k))
-            own[e] = k
-            load[k] += len(toks[r][e])
-        teams.append(team)
-        owner.append(own)
-    return cores, toks, col, total, teams, owner
-
-
-def _runs(ts):
+def runs(ts):
     out = []
     for t in ts:
         if out and out[-1][0] + out[-1][1] == t:
@@ -62,8 +29,103 @@ def _runs(ts):
     return out
 
 
+def share(cores, toks, teams, topo):
+    n = len(cores)
+    power = 16
+
+    def can(r, k, e):
+        if e == r and not topo.may_write(cores[r], cores[r] ^ 8):
+            return k == cores[r]
+        return k == cores[e] or topo.may_write(k, cores[e])
+
+    def loads(r, e, k):
+        a, b, d = topo.chip(k), topo.chip(cores[e]), topo.die(k)
+        w = len(toks[r][e])
+        out = [(("work", k), len(runs(toks[r][e])) + (1 if k != cores[e] else 0))]
+        if (a ^ b) & 1:
+            out.append((("mate", a, d), w))
+            a ^= 1
+        if a != b:
+            out.append((("port", "out", a, d), w))
+            out.append((("port", "in", b, d), w))
+        return out
+
+    load = {}
+    for r in range(n):
+        for k in teams[r]:
+            for e in range(n):
+                if can(r, k, e):
+                    for l, w in loads(r, e, k):
+                        load[l] = 0
+    for r in range(n):
+        load[("work", cores[r])] = 5
+    owner = [[None] * n for r in range(n)]
+    for r in range(n):
+        for e in sorted(range(n), key=lambda e: (sum(can(r, k, e) for k in teams[r]), -len(toks[r][e]), e)):
+            k = min((k for k in teams[r] if can(r, k, e)), key=lambda k: (load[("work", k)], k))
+            owner[r][e] = k
+            for l, w in loads(r, e, k):
+                load[l] += w
+    mean = {}
+    for kind in ("work", "mate", "port"):
+        vals = [v for l, v in load.items() if l[0] == kind]
+        mean[kind] = max(1.0, sum(vals) / max(1, len(vals)))
+
+    again, sweeps = True, 0
+    while again and sweeps < 30:
+        again = False
+        sweeps += 1
+        for r in range(n):
+            for e in range(n):
+                for f in [None] + list(range(e + 1, n)):
+                    for b in (teams[r] if f is None else [owner[r][f]]):
+                        a = owner[r][e]
+                        if b == a or not can(r, b, e) or (f is not None and not can(r, a, f)):
+                            continue
+                        delta = {}
+                        for l, w in loads(r, e, b) + ([] if f is None else loads(r, f, a)):
+                            delta[l] = delta.get(l, 0) + w
+                        for l, w in loads(r, e, a) + ([] if f is None else loads(r, f, b)):
+                            delta[l] = delta.get(l, 0) - w
+                        gain = 0.0
+                        for l, w in delta.items():
+                            gain += ((load[l] + w) / mean[l[0]]) ** power - (load[l] / mean[l[0]]) ** power
+                        if gain < -1e-9:
+                            for l, w in delta.items():
+                                load[l] += w
+                            owner[r][e] = b
+                            if f is not None:
+                                owner[r][f] = a
+                            again = True
+    return owner
+
+
+def plan(T, topo):
+    if "plan" in CACHE:
+        return CACHE["plan"]
+    route = T.tables["ROUTE"]
+    cores = list(T.cores)
+    n = len(cores)
+    toks = [[[] for e in range(n)] for r in range(n)]
+    for r in range(n):
+        for t, es in enumerate(route[r]):
+            toks[r][es[0]].append(t)
+    col = [[0] * n for r in range(n)]
+    total = [0] * n
+    for e in range(n):
+        for r in range(n):
+            col[r][e] = total[e]
+            total[e] += len(toks[r][e])
+    teams = []
+    for c in cores:
+        teams.append([c - c % 8 + (c + 2 * i) % 8 for i in range(4)])
+    owner = share(cores, toks, teams, topo)
+    CACHE["plan"] = (cores, toks, col, total, teams, owner)
+    return CACHE["plan"]
+
+
 def rank_program(g, core, T, topo):
-    cores, toks, col, total, teams, owner = _plan(T, topo)
+    cores, toks, col, total, teams, owner = plan(T, topo)
     n = len(cores)
     src = [r for r in range(n) if core in teams[r]]
     if not src:
@@ -82,7 +144,7 @@ def rank_program(g, core, T, topo):
         helpers = [k for k in teams[r] if k != core]
         ids = [DstId(rid=topo.addr(k)[0], pnc=topo.addr(k)[1]) for k in helpers]
         g.remote_dma_fused([RemoteDMATransfer(dst_ids=ids, dma_engine_mask=0xFFFF, remote_sem=sem.xin,
-                                              srcs=[T.xs[:]], dsts=[T.xs[:] for _ in helpers])],
+                                              srcs=[T.xs[:]], dsts=[T.xs[:] for k in helpers])],
                            local_sem=sem.sent)
         sent += 16
     else:
@@ -94,24 +156,21 @@ def rank_program(g, core, T, topo):
     blocks = []
     pos, turn = 0, 0
     for i, e in enumerate(mine):
-        ng = nh = 0
         local = cores[e] == core
-        at = col[r][e] if local else pos
+        first = col[r][e] if local else pos
         buf = T.land if local else T.pack
-        first = at
-        for t, ln in _runs(toks[r][e]):
+        at = first
+        count = [0, 0]
+        for t, ln in runs(toks[r][e]):
             q = queues[turn % 3]
             turn += 1
-            if q is g:
-                q.dma_start(buf[:, at:at + ln], T.xs[:, t:t + ln]).then_inc(sem["pg%d" % i], 16)
-                ng += 1
-            else:
-                q.dma_start(buf[:, at:at + ln], T.xs[:, t:t + ln]).then_inc(sem["ph%d" % i], 16)
-                nh += 1
+            own_g = 1 if q is g else 0
+            q.dma_start(buf[:, at:at + ln], T.xs[:, t:t + ln]).then_inc(sem[("pg%d" if own_g else "ph%d") % i], 16)
+            count[own_g] += 1
             at += ln
         if not local:
             pos = at
-        blocks.append((e, first, ng, nh))
+        blocks.append((e, first, count[1], count[0]))
 
     for i, (e, first, ng, nh) in enumerate(blocks):
         if ng:
@@ -122,18 +181,18 @@ def rank_program(g, core, T, topo):
         if dst == core:
             continue
         w = len(toks[r][e])
-        rid, pid, _se = topo.addr(dst)
+        rid, pid = topo.addr(dst)[0:2]
         m = topo.mask(core, dst)
         g.remote_dma(T.land[:, col[r][e]:col[r][e] + w], T.pack[:, first:first + w],
                      sem.arr, sem.sent, pid, rid, m)
-        sent += _engines(m)
+        sent += engines(m)
 
     if me is not None:
         need = 0
         for s in range(n):
             k = owner[s][me]
             if toks[s][me] and k != core:
-                need += _engines(topo.mask(k, core))
+                need += engines(topo.mask(k, core))
         if need:
             g.wait_ge(sem.arr, need)
         g.dma_start(T.y[:, 0:total[me]], T.land[:, 0:total[me]]).then_inc(sem.st, 16)

from concourse.bass import DstId, RemoteDMATransfer

NTOK = 512
YW = 561
MAXB = 10

SCRATCH = {
    "xs": ("sbuf", [128, NTOK], "bfloat16"),
    "pack": ("sbuf", [128, NTOK], "bfloat16"),
    "land": ("sbuf", [128, YW], "bfloat16"),
}
SEMAPHORES = (["ld", "xin", "sent", "arr", "st"] + ["pg%d" % i for i in range(MAXB)]
              + ["ph%d" % i for i in range(MAXB)])

CACHE = {}


def engines(mask):
    return bin(mask).count("1")


def runs(ts):
    out = []
    for t in ts:
        if out and out[-1][0] + out[-1][1] == t:
            out[-1][1] += 1
        else:
            out.append([t, 1])
    return out


def share(cores, toks, teams, topo):
    n = len(cores)
    power = 16

    def can(r, k, e):
        if e == r and not topo.may_write(cores[r], cores[r] ^ 8):
            return k == cores[r]
        return k == cores[e] or topo.may_write(k, cores[e])

    def loads(r, e, k):
        a, b, d = topo.chip(k), topo.chip(cores[e]), topo.die(k)
        w = len(toks[r][e])
        out = [(("work", k), len(runs(toks[r][e])) + (1 if k != cores[e] else 0))]
        if (a ^ b) & 1:
            out.append((("mate", a, d), w))
            a ^= 1
        if a != b:
            out.append((("port", "out", a, d), w))
            out.append((("port", "in", b, d), w))
        return out

    load = {}
    for r in range(n):
        for k in teams[r]:
            for e in range(n):
                if can(r, k, e):
                    for l, w in loads(r, e, k):
                        load[l] = 0
    for r in range(n):
        load[("work", cores[r])] = 5
    owner = [[None] * n for r in range(n)]
    for r in range(n):
        for e in sorted(range(n), key=lambda e: (sum(can(r, k, e) for k in teams[r]), -len(toks[r][e]), e)):
            k = min((k for k in teams[r] if can(r, k, e)), key=lambda k: (load[("work", k)], k))
            owner[r][e] = k
            for l, w in loads(r, e, k):
                load[l] += w
    mean = {}
    for kind in ("work", "mate", "port"):
        vals = [v for l, v in load.items() if l[0] == kind]
        mean[kind] = max(1.0, sum(vals) / max(1, len(vals)))

    again, sweeps = True, 0
    while again and sweeps < 30:
        again = False
        sweeps += 1
        for r in range(n):
            for e in range(n):
                for f in [None] + list(range(e + 1, n)):
                    for b in (teams[r] if f is None else [owner[r][f]]):
                        a = owner[r][e]
                        if b == a or not can(r, b, e) or (f is not None and not can(r, a, f)):
                            continue
                        delta = {}
                        for l, w in loads(r, e, b) + ([] if f is None else loads(r, f, a)):
                            delta[l] = delta.get(l, 0) + w
                        for l, w in loads(r, e, a) + ([] if f is None else loads(r, f, b)):
                            delta[l] = delta.get(l, 0) - w
                        gain = 0.0
                        for l, w in delta.items():
                            gain += ((load[l] + w) / mean[l[0]]) ** power - (load[l] / mean[l[0]]) ** power
                        if gain < -1e-9:
                            for l, w in delta.items():
                                load[l] += w
                            owner[r][e] = b
                            if f is not None:
                                owner[r][f] = a
                            again = True
    return owner


def plan(T, topo):
    if "plan" in CACHE:
        return CACHE["plan"]
    route = T.tables["ROUTE"]
    cores = list(T.cores)
    n = len(cores)
    toks = [[[] for e in range(n)] for r in range(n)]
    for r in range(n):
        for t, es in enumerate(route[r]):
            toks[r][es[0]].append(t)
    col = [[0] * n for r in range(n)]
    total = [0] * n
    for e in range(n):
        for r in range(n):
            col[r][e] = total[e]
            total[e] += len(toks[r][e])
    teams = []
    for c in cores:
        teams.append([c - c % 8 + (c + 2 * i) % 8 for i in range(4)])
    owner = share(cores, toks, teams, topo)
    CACHE["plan"] = (cores, toks, col, total, teams, owner)
    return CACHE["plan"]


def rank_program(g, core, T, topo):
    cores, toks, col, total, teams, owner = plan(T, topo)
    n = len(cores)
    src = [r for r in range(n) if core in teams[r]]
    if not src:
        return
    r = src[0]
    lead = cores[r]
    me = T.rank_of(core)
    sem = T.sem
    queues = [g.sync, g.scalar, g]
    sent = 0

    if core == lead:
        g.sync.dma_start(T.xs[:], T.x[:]).then_inc(sem.ld, 16)
        for q in queues:
            q.wait_ge(sem.ld, 16)
        helpers = [k for k in teams[r] if k != core]
        ids = [DstId(rid=topo.addr(k)[0], pnc=topo.addr(k)[1]) for k in helpers]
        g.remote_dma_fused([RemoteDMATransfer(dst_ids=ids, dma_engine_mask=0xFFFF, remote_sem=sem.xin,
                                              srcs=[T.xs[:]], dsts=[T.xs[:] for k in helpers])],
                           local_sem=sem.sent)
        sent += 16
    else:
        for q in queues:
            q.wait_ge(sem.xin, 16)

    mine = [e for e in range(n) if owner[r][e] == core and toks[r][e]]
    mine.sort(key=lambda e: (cores[e] == core, topo.chip(cores[e]) == topo.chip(core), e))
    blocks = []
    pos, turn = 0, 0
    for i, e in enumerate(mine):
        local = cores[e] == core
        first = col[r][e] if local else pos
        buf = T.land if local else T.pack
        at = first
        count = [0, 0]
        for t, ln in runs(toks[r][e]):
            q = queues[turn % 3]
            turn += 1
            own_g = 1 if q is g else 0
            q.dma_start(buf[:, at:at + ln], T.xs[:, t:t + ln]).then_inc(sem[("pg%d" if own_g else "ph%d") % i], 16)
            count[own_g] += 1
            at += ln
        if not local:
            pos = at
        blocks.append((e, first, count[1], count[0]))

    for i, (e, first, ng, nh) in enumerate(blocks):
        if ng:
            g.wait_ge(sem["pg%d" % i], 16 * ng)
        if nh:
            g.wait_ge(sem["ph%d" % i], 16 * nh)
        dst = cores[e]
        if dst == core:
            continue
        w = len(toks[r][e])
        rid, pid = topo.addr(dst)[0:2]
        m = topo.mask(core, dst)
        g.remote_dma(T.land[:, col[r][e]:col[r][e] + w], T.pack[:, first:first + w],
                     sem.arr, sem.sent, pid, rid, m)
        sent += engines(m)

    if me is not None:
        need = 0
        for s in range(n):
            k = owner[s][me]
            if toks[s][me] and k != core:
                need += engines(topo.mask(k, core))
        if need:
            g.wait_ge(sem.arr, need)
        g.dma_start(T.y[:, 0:total[me]], T.land[:, 0:total[me]]).then_inc(sem.st, 16)
        g.wait_ge(sem.st, 16)
    if sent:
        g.wait_ge(sem.sent, sent)
